import numpy as np
import ml_dtypes


def mxq(x, axis, fmt="e4m3"):
    dtype, down = {"e4m3": (ml_dtypes.float8_e4m3fn, 7), "e5m2": (ml_dtypes.float8_e5m2, 14)}[fmt]
    v = np.moveaxis(np.asarray(x, np.float32).astype(ml_dtypes.bfloat16).astype(np.float64), axis, -1)
    blocks = v.reshape(v.shape[:-1] + (-1, 32))
    amax = np.abs(blocks).max(-1, keepdims=True)
    byte = np.maximum(np.where(amax > 0, np.frexp(amax)[1] - 1 + 127, 0) - down, 1)
    scale = np.exp2(byte - 127.0)
    codes = (blocks / scale).astype(np.float32).astype(dtype).astype(np.float64)
    return np.moveaxis((codes * scale).reshape(v.shape), -1, axis)


WIDE = False


def mx_kscale(k):
    if not WIDE:
        return np.ones(k)
    levels = np.array([30, -30])
    if k % 512:
        return np.exp2(np.random.permutation(np.resize(levels, k // 32))).repeat(32)
    a = np.empty((k // 512, 16))
    for p in range(k // 512):
        a[p, :8] = np.random.permutation(np.resize(levels, 8))
        for g in range(8):
            far = levels[np.abs(levels - a[p, g]) >= 10]
            a[p, g + 8] = far[np.random.randint(len(far))]
    return np.exp2(a.ravel()).repeat(32)


def f64(x):
    return np.asarray(x).astype(np.float64)


E2M1 = np.array([0.0, 0.5, 1.0, 1.5, 2.0, 3.0, 4.0, 6.0, -0.0, -0.5, -1.0, -1.5, -2.0, -3.0, -4.0, -6.0])


def pack_weight(w, fmt):
    k, n = w.shape
    w = f64(np.asarray(w, np.float32).astype(ml_dtypes.bfloat16)).reshape(k // 32, 32, n)
    amax = np.abs(w).max(1)
    if fmt == "e4m3":
        byte = np.frexp(amax)[1] - 1 + 127 - 7
    else:
        mant, ex = np.frexp(amax / 6.0)
        byte = np.where(mant > 0.5, ex, ex - 1) + 127
    byte = np.clip(np.where(amax > 0, byte, 1), 1, 254)
    scaled = (w * np.exp2(127.0 - byte)[:, None, :]).reshape(k, n).astype(np.float32)
    by_word = np.ascontiguousarray(scaled.reshape(k // 512, 128, 4, n).transpose(0, 1, 3, 2))
    if fmt == "e4m3":
        words = by_word.astype(ml_dtypes.float8_e4m3fn).view(np.uint8)
    else:
        c = by_word.astype(ml_dtypes.float4_e2m1fn).view(np.uint8) & 0xF
        words = (c[..., 0::2] | (c[..., 1::2] << 4)).reshape(k // 512, 128, 2 * n)
    return np.ascontiguousarray(words), np.ascontiguousarray(byte.astype(np.uint8).reshape(k // 512, 16, n))


def unpack_weight(words, scales, fmt):
    g, _, n = scales.shape
    words = np.ascontiguousarray(words).reshape(g, 128, n, -1)
    if fmt == "e4m3":
        vals = words.view(ml_dtypes.float8_e4m3fn).astype(np.float64)
    else:
        nib = np.empty((g, 128, n, 4), np.uint8)
        nib[..., 0::2] = words & 0xF
        nib[..., 1::2] = words >> 4
        vals = E2M1[nib]
    vals = vals * np.repeat(np.exp2(scales.astype(np.float64) - 127.0), 8, axis=1)[..., None]
    return vals.transpose(0, 1, 3, 2).reshape(g * 512, n)


def bf(x):
    return np.asarray(x, np.float32).astype(ml_dtypes.bfloat16)


def planes(Y):
    r, m = Y.shape
    b = f64(bf(Y)).reshape(r // 32, 32, m)
    amax = np.abs(b).max(1)
    byte = np.clip(np.where(amax > 0, np.frexp(amax)[1] - 1 + 127 - 7, 1), 1, 254)
    codes = (b * np.exp2(127.0 - byte)[:, None, :]).reshape(r, m).astype(np.float32).astype(ml_dtypes.float8_e4m3fn).view(np.uint8)
    words = codes.reshape(r // 512, 128, 4, m).transpose(0, 1, 3, 2)
    return np.ascontiguousarray(words), np.ascontiguousarray(byte.astype(np.uint8).reshape(r // 512, 16, m))


N, L, R, K, T = 512, 1024, 512, 512, 512


def setup_inputs():
    n = np.random.standard_normal
    fn = mx_kscale(N)
    fl = mx_kscale(L)
    fr = mx_kscale(R)
    wdp = pack_weight(n((N, R)) * 1 / np.sqrt(N) * fn[:, None], "e4m3")
    xqp = pack_weight(n((L, T)) / fl[:, None], "e2m1")
    wsp = pack_weight(n((L, R)) * 1 / np.sqrt(L) * fl[:, None], "e4m3")
    wup = pack_weight(n((R, K)) * 1 / np.sqrt(R) / fr[:, None], "e2m1")
    return {
        "g": (n((N, T)) * np.exp(0.5 * n((1, T))) / fn[:, None]).astype(np.float32),
        "wd_words": wdp[0],
        "wd_scales": wdp[1],
        "xq_words": xqp[0],
        "xq_scales": xqp[1],
        "ws_words": wsp[0],
        "ws_scales": wsp[1],
        "us": (np.random.uniform(0.5, 2.0, (R, 1)) * fr[:, None]).astype(np.float32),
        "wu_words": wup[0],
        "wu_scales": wup[1],
    }


def reference(g, wd_words, wd_scales, xq_words, xq_scales, ws_words, ws_scales, us, wu_words, wu_scales):
    wdu = unpack_weight(wd_words, wd_scales, "e4m3")
    xqu = unpack_weight(xq_words, xq_scales, "e2m1")
    wsu = unpack_weight(ws_words, ws_scales, "e4m3")
    wuu = unpack_weight(wu_words, wu_scales, "e2m1")
    gq = mxq(f64(g), 0, "e5m2")
    d = wdu.T @ gq + wsu.T @ xqu
    dc = np.maximum(np.minimum(d, 1.0), 0.0 - 1.0) * f64(us)
    dcq = mxq(dc, 0, "e5m2")
    y = wuu.T @ dcq
    words, scales = planes(y)
    return y, words, scales

@@ -1,0 +1,261 @@
+from contextlib import ExitStack
+
+import concourse.mybir as mybir
+
+N, L, R, K, T = 512, 1024, 512, 512, 512
+FLOPS = 2 * T * (N * R + L * R + R * K)
+
+F32 = mybir.dt.float32
+BF16 = mybir.dt.bfloat16
+I32 = mybir.dt.int32
+U8 = mybir.dt.uint8
+E4M3 = mybir.dt.float8_e4m3fn_x4
+E5M2 = mybir.dt.float8_e5m2_x4
+E2M1 = mybir.dt.float4_e2m1fn_x4
+ALU = mybir.AluOpType
+ACT = mybir.ActivationFunctionType
+
+P = 128
+PACK = 4
+HALF = T // 2
+RUN = 4
+G_VECTOR_COLS = 176
+
+
+def tile_mix_gradient_clipped_between_pl_kernel(
+    tc, g, wd_words, wd_scales, xq_words, xq_scales, ws_words, ws_scales, us, wu_words, wu_scales,
+    out_0, out_1, out_2,
+):
+    nc = tc.nc
+
+    with ExitStack() as ctx:
+        sb = ctx.enter_context(tc.tile_pool(name="sb", bufs=1))
+        ps = ctx.enter_context(tc.psum_pool(name="ps", bufs=1))
+        ctx.enter_context(tc.manual_schedule())
+
+        def tile(name, shape, dtype):
+            return sb.tile(shape, dtype, name=name, align_bytes=64)
+
+        def load_scale_rows(engine, plane, scales, q):
+            passes = scales.shape[0]
+            engine.dma_start(
+                out=plane[32 * q : 32 * q + 4, :].bitcast(I32).rearrange("r (z c) -> r z c", z=passes),
+                in_=scales[:, 4 * q : 4 * q + 4, :].bitcast(I32).rearrange("z r c -> r z c"),
+            )
+
+        def interleave(copy, dst, src, c0, c1):
+            copy(
+                out=dst[:, PACK * c0 : PACK * c1].rearrange("p (c i j) -> p c j i", i=RUN, j=PACK),
+                in_=src[:, :, c0:c1].rearrange("p j (c i) -> p c j i", i=RUN),
+            )
+
+        def deal_words(dst, src):
+            nc.vector.tensor_copy(
+                out=dst.rearrange("p (j c i) -> p c j i", j=PACK, i=RUN),
+                in_=src.rearrange("p (c i j) -> p c j i", j=PACK, i=RUN),
+            )
+
+        def deal_scales(dst, src):
+            nc.vector.tensor_copy(
+                out=dst.rearrange("p (z j m) -> p z j m", j=PACK, m=P),
+                in_=src.rearrange("p (z m j) -> p z j m", j=PACK, m=P),
+            )
+
+        ws_scale_raw = tile("ws_scale_raw", [P, 2 * R], U8)
+        xq_scale = tile("xq_scale", [P, 2 * T], U8)
+        wd_scale_raw = tile("wd_scale_raw", [P, R], U8)
+        wu_scale_raw = tile("wu_scale_raw", [P, K], U8)
+        dc_codes = tile("dc_codes", [P, HALF + T], I32)
+        dc_scale = tile("dc_scale", [P, HALF + T], U8)
+        us_cols = tile("us_cols", [P, PACK], F32)
+        ws_raw = tile("ws_raw", [P, 2 * R], I32)
+        xq_codes = tile("xq_codes", [P, 4 * T], U8)
+        wd_raw = tile("wd_raw", [P, R], I32)
+        wu_raw = tile("wu_raw", [P, 2 * K], U8)
+        g_raw = [tile("g_raw%d" % h, [P, PACK, HALF], F32) for h in range(2)]
+
+        for plane in (ws_scale_raw, xq_scale, wd_scale_raw, wu_scale_raw):
+            nc.vector.memset(plane[:].bitcast(I32), 0)
+        nc.vector.memset(dc_codes[:, :HALF], 0)
+        nc.vector.memset(dc_scale[:, :HALF].bitcast(I32), 0)
+
+        nc.gpsimd.dma_start(out=us_cols[:], in_=us.rearrange("(p j) o -> p (j o)", j=PACK))
+        for q in range(4):
+            load_scale_rows(nc.scalar, ws_scale_raw, ws_scales, q)
+        nc.sync.dma_start(
+            out=ws_raw[:].rearrange("p (z c) -> p z c", z=2),
+            in_=ws_words.rearrange("z p c j -> p z (c j)").bitcast(I32),
+        )
+        nc.sync.dma_start(
+            out=xq_codes[:].bitcast(I32).rearrange("p (z c) -> p z c", z=2),
+            in_=xq_words.rearrange("z p b -> p z b").bitcast(I32),
+        )
+        for q in range(2):
+            load_scale_rows(nc.sync, xq_scale, xq_scales, q)
+        for q in range(2, 4):
+            load_scale_rows(nc.scalar, xq_scale, xq_scales, q)
+        for q in range(4):
+            load_scale_rows(nc.gpsimd, wd_scale_raw, wd_scales, q)
+        g_rows = g.rearrange("(p j) t -> p j t", j=PACK)
+        for h in range(2):
+            nc.sync.dma_start(out=g_raw[h][:], in_=g_rows[:, :, h * HALF : (h + 1) * HALF])
+        nc.sync.dma_start(out=wd_raw[:], in_=wd_words[0].rearrange("p c j -> p (c j)").bitcast(I32))
+        nc.sync.dma_start(out=wu_raw[:].bitcast(I32), in_=wu_words[0].bitcast(I32))
+        for q in range(4):
+            load_scale_rows(nc.sync, wu_scale_raw, wu_scales, q)
+
+        upper = tile("upper", [P, PACK], F32)
+        lower = tile("lower", [P, PACK], F32)
+        nc.scalar.activation(out=upper[:], in_=us_cols[:], func=ACT.Abs)
+        nc.scalar.activation(out=lower[:], in_=upper[:], func=ACT.Copy, scale=-1.0)
+
+        ws_scale = tile("ws_scale", [P, 2 * R], U8)
+        deal_scales(ws_scale[:], ws_scale_raw[:])
+        ws_codes = [tile("ws_codes%d" % z, [P, R], I32) for z in range(2)]
+        for z in range(2):
+            deal_words(ws_codes[z][:], ws_raw[:, z * R : (z + 1) * R])
+
+        d = [ps.tile([P, T], F32, name="d%d" % j, tag="bank%d" % j) for j in range(PACK)]
+        for z in range(2):
+            for j in range(PACK):
+                nc.tensor.matmul_mx(
+                    out=d[j][:],
+                    lhsT=ws_codes[z][:, j * P : (j + 1) * P].bitcast(E4M3),
+                    lhsT_scale=ws_scale[:, z * R + j * P : z * R + (j + 1) * P],
+                    rhs=xq_codes[:, 2 * z * T : 2 * (z + 1) * T].bitcast(E2M1),
+                    rhs_scale=xq_scale[:, z * T : (z + 1) * T],
+                    start=(z == 0),
+                    stop=False,
+                )
+
+        g_bf = [tile("g_bf%d" % h, [P, PACK * HALF], BF16) for h in range(2)]
+        g_codes = tile("g_codes", [P, T], I32)
+        g_scale = tile("g_scale", [P, T], U8)
+        wd_scale = tile("wd_scale", [P, R], U8)
+        wd_codes = tile("wd_codes", [P, R], I32)
+
+        def round_g(h):
+            interleave(nc.vector.tensor_copy, g_bf[h], g_raw[h], 0, G_VECTOR_COLS)
+            interleave(nc.scalar.copy, g_bf[h], g_raw[h], G_VECTOR_COLS, HALF)
+
+        def quantize_g(h):
+            cols = slice(h * HALF, (h + 1) * HALF)
+            nc.vector.quantize_mx(out=g_codes[:, cols].bitcast(E5M2), scales=g_scale[:, cols], in_=g_bf[h][:])
+
+        round_g(0)
+        deal_scales(wd_scale[:], wd_scale_raw[:])
+        quantize_g(0)
+        round_g(1)
+        deal_words(wd_codes[:], wd_raw[:])
+        quantize_g(1)
+
+        for j in range(PACK):
+            nc.tensor.matmul_mx(
+                out=d[j][:],
+                lhsT=wd_codes[:, j * P : (j + 1) * P].bitcast(E4M3),
+                lhsT_scale=wd_scale[:, j * P : (j + 1) * P],
+                rhs=g_codes[:].bitcast(E5M2),
+                rhs_scale=g_scale[:],
+                start=False,
+                stop=True,
+            )
+
+        wu_scale = tile("wu_scale", [P, K], U8)
+        wu_codes = tile("wu_codes", [P, 2 * K], U8)
+        nc.vector.tensor_copy(
+            out=wu_codes[:].rearrange("p (j m b) -> p j m b", j=PACK, b=2),
+            in_=wu_raw[:].rearrange("p (m j b) -> p j m b", j=PACK, b=2),
+        )
+        deal_scales(wu_scale[:], wu_scale_raw[:])
+
+        product = [[tile("product%d%d" % (h, j), [P, HALF], BF16) for j in range(PACK)] for h in range(2)]
+        dc_rows = [tile("dc_rows%d" % h, [P, PACK, HALF], BF16) for h in range(2)]
+        dc_bf = [tile("dc_bf%d" % h, [P, PACK * HALF], BF16) for h in range(2)]
+
+        def scale_on_scalar(h, j):
+            nc.scalar.activation(
+                out=product[h][j][:], in_=d[j][:, h * HALF : (h + 1) * HALF], func=ACT.Copy, scale=us_cols[:, j : j + 1]
+            )
+
+        def scale_on_vector(h, j):
+            nc.vector.tensor_scalar(
+                out=product[h][j][:], in0=d[j][:, h * HALF : (h + 1) * HALF],
+                scalar1=us_cols[:, j : j + 1], scalar2=None, op0=ALU.mult,
+            )
+
+        def clip(h, j):
+            nc.vector.tensor_scalar(
+                out=dc_rows[h][:, j, :], in0=product[h][j][:],
+                scalar1=upper[:, j : j + 1], scalar2=lower[:, j : j + 1], op0=ALU.min, op1=ALU.max,
+            )
+
+        def quantize_dc(h):
+            cols = slice((h + 1) * HALF, (h + 2) * HALF)
+            nc.vector.quantize_mx(out=dc_codes[:, cols].bitcast(E5M2), scales=dc_scale[:, cols], in_=dc_bf[h][:])
+
+        scale_on_scalar(0, 0)
+        scale_on_vector(0, 1)
+        scale_on_scalar(1, 0)
+        scale_on_scalar(0, 2)
+        clip(0, 0)
+        clip(0, 1)
+        scale_on_vector(0, 3)
+        scale_on_scalar(1, 1)
+        scale_on_scalar(1, 2)
+        scale_on_scalar(1, 3)
+        clip(0, 2)
+        clip(0, 3)
+        clip(1, 0)
+        interleave(nc.vector.tensor_copy, dc_bf[0], dc_rows[0], 0, HALF)
+        clip(1, 1)
+        quantize_dc(0)
+        clip(1, 2)
+        clip(1, 3)
+
+        def last_product(h):
+            banks = [ps.tile([P, T], F32, name="y%d%d" % (h, i), tag="bank%d" % (PACK * (1 - h) + i)) for i in range(PACK)]
+            cols = slice(h * HALF, h * HALF + T)
+            for i in range(PACK):
+                nc.tensor.matmul_mx(
+                    out=banks[i][:],
+                    lhsT=wu_codes[:, 2 * i * P : 2 * (i + 1) * P].bitcast(E2M1),
+                    lhsT_scale=wu_scale[:, i * P : (i + 1) * P],
+                    rhs=dc_codes[:, cols].bitcast(E5M2),
+                    rhs_scale=dc_scale[:, cols],
+                    start=True,
+                    stop=True,
+                )
+            return banks
+
+        y_rows = [tile("y_rows%d" % h, [P, PACK, HALF], F32) for h in range(2)]
+        y_bf = [tile("y_bf%d" % h, [P, PACK * HALF], BF16) for h in range(2)]
+        y_codes = [tile("y_codes%d" % h, [P, HALF], I32) for h in range(2)]
+        y_scale = tile("y_scale", [P, T], U8)
+        out_rows = out_0.rearrange("(p i) t -> p i t", i=PACK)
+        out_words = out_1[0].rearrange("p c j -> p (c j)").bitcast(I32)
+
+        def empty_banks(h, banks):
+            for i in range(PACK):
+                nc.scalar.copy(out=y_rows[h][:, i, :], in_=banks[i][:, HALF:])
+            nc.sync.dma_start(out=out_rows[:, :, h * HALF : (h + 1) * HALF], in_=y_rows[h][:])
+
+        def hand_on(h):
+            cols = slice(h * HALF, (h + 1) * HALF)
+            interleave(nc.vector.tensor_copy, y_bf[h], y_rows[h], 0, HALF)
+            nc.vector.quantize_mx(out=y_codes[h][:].bitcast(E4M3), scales=y_scale[:, cols], in_=y_bf[h][:])
+            nc.sync.dma_start(out=out_words[:, cols], in_=y_codes[h][:])
+
+        first = last_product(0)
+        interleave(nc.vector.tensor_copy, dc_bf[1], dc_rows[1], 0, HALF)
+        quantize_dc(1)
+        second = last_product(1)
+        empty_banks(0, first)
+        hand_on(0)
+        empty_banks(1, second)
+        hand_on(1)
+        for q in range(4):
+            engine = nc.scalar if q % 2 else nc.sync
+            engine.dma_start(
+                out=out_2[0, 4 * q : 4 * q + 4, :].bitcast(I32),
+                in_=y_scale[32 * q : 32 * q + 4, :].bitcast(I32),
+            )

@@ -79,35 +79,30 @@ def tile_mix_gradient_clipped_between_pl_kernel(
         nc.vector.memset(dc_codes[:, :HALF], 0)
         nc.vector.memset(dc_scale[:, :HALF].bitcast(I32), 0)
 
-        nc.gpsimd.dma_start(out=us_cols[:], in_=us.rearrange("(p j) o -> p (j o)", j=PACK))
-        for q in range(4):
-            load_scale_rows(nc.scalar, ws_scale_raw, ws_scales, q)
-        nc.sync.dma_start(
-            out=ws_raw[:].rearrange("p (z c) -> p z c", z=2),
-            in_=ws_words.rearrange("z p c j -> p z (c j)").bitcast(I32),
-        )
         nc.sync.dma_start(
             out=xq_codes[:].bitcast(I32).rearrange("p (z c) -> p z c", z=2),
             in_=xq_words.rearrange("z p b -> p z b").bitcast(I32),
         )
-        for q in range(2):
-            load_scale_rows(nc.sync, xq_scale, xq_scales, q)
-        for q in range(2, 4):
-            load_scale_rows(nc.scalar, xq_scale, xq_scales, q)
         for q in range(4):
-            load_scale_rows(nc.gpsimd, wd_scale_raw, wd_scales, q)
+            load_scale_rows(nc.scalar if q % 2 else nc.sync, ws_scale_raw, ws_scales, q)
+        for q in range(2):
+            load_scale_rows(nc.scalar if q % 2 else nc.sync, xq_scale, xq_scales, q)
+        nc.sync.dma_start(
+            out=ws_raw[:].rearrange("p (z c) -> p z c", z=2),
+            in_=ws_words.rearrange("z p c j -> p z (c j)").bitcast(I32),
+        )
+        for q in range(2, 4):
+            load_scale_rows(nc.sync, xq_scale, xq_scales, q)
         g_rows = g.rearrange("(p j) t -> p j t", j=PACK)
-        for h in range(2):
-            nc.sync.dma_start(out=g_raw[h][:], in_=g_rows[:, :, h * HALF : (h + 1) * HALF])
+        nc.sync.dma_start(out=g_raw[0][:], in_=g_rows[:, :, :HALF])
+        for q in range(4):
+            load_scale_rows(nc.sync, wd_scale_raw, wd_scales, q)
+        nc.sync.dma_start(out=g_raw[1][:], in_=g_rows[:, :, HALF:])
         nc.sync.dma_start(out=wd_raw[:], in_=wd_words[0].rearrange("p c j -> p (c j)").bitcast(I32))
+        nc.sync.dma_start(out=us_cols[:], in_=us.rearrange("(p j) o -> p (j o)", j=PACK))
         nc.sync.dma_start(out=wu_raw[:].bitcast(I32), in_=wu_words[0].bitcast(I32))
         for q in range(4):
             load_scale_rows(nc.sync, wu_scale_raw, wu_scales, q)
-
-        upper = tile("upper", [P, PACK], F32)
-        lower = tile("lower", [P, PACK], F32)
-        nc.scalar.activation(out=upper[:], in_=us_cols[:], func=ACT.Abs)
-        nc.scalar.activation(out=lower[:], in_=upper[:], func=ACT.Copy, scale=-1.0)
 
         ws_scale = tile("ws_scale", [P, 2 * R], U8)
         deal_scales(ws_scale[:], ws_scale_raw[:])
@@ -134,18 +129,22 @@ def tile_mix_gradient_clipped_between_pl_kernel(
         wd_scale = tile("wd_scale", [P, R], U8)
         wd_codes = tile("wd_codes", [P, R], I32)
 
-        def round_g(h):
-            interleave(nc.vector.tensor_copy, g_bf[h], g_raw[h], 0, G_VECTOR_COLS)
-            interleave(nc.scalar.copy, g_bf[h], g_raw[h], G_VECTOR_COLS, HALF)
+        def cast_on_scalar(out, in_):
+            nc.scalar.activation(out=out, in_=in_, func=ACT.Copy)
+
+        def interleave_shared(dst, src):
+            interleave(nc.vector.tensor_copy, dst, src, 0, G_VECTOR_COLS)
+            interleave(nc.scalar.copy, dst, src, G_VECTOR_COLS, HALF)
 
         def quantize_g(h):
             cols = slice(h * HALF, (h + 1) * HALF)
             nc.vector.quantize_mx(out=g_codes[:, cols].bitcast(E5M2), scales=g_scale[:, cols], in_=g_bf[h][:])
 
-        round_g(0)
+        interleave(nc.vector.tensor_copy, g_bf[0], g_raw[0], 0, G_VECTOR_COLS)
+        interleave(cast_on_scalar, g_bf[0], g_raw[0], G_VECTOR_COLS, HALF)
         deal_scales(wd_scale[:], wd_scale_raw[:])
         quantize_g(0)
-        round_g(1)
+        interleave_shared(g_bf[1], g_raw[1])
         deal_words(wd_codes[:], wd_raw[:])
         quantize_g(1)
 
@@ -157,6 +156,23 @@ def tile_mix_gradient_clipped_between_pl_kernel(
                 rhs=g_codes[:].bitcast(E5M2),
                 rhs_scale=g_scale[:],
                 start=False,
+                stop=True,
+            )
+
+        upper = tile("upper", [P, PACK], F32)
+        lower = tile("lower", [P, PACK], F32)
+        nc.scalar.activation(out=upper[:], in_=us_cols[:], func=ACT.Abs)
+        nc.scalar.activation(out=lower[:], in_=upper[:], func=ACT.Copy, scale=-1.0)
+
+        y_banks = [ps.tile([P, T], F32, name="y0%d" % i, tag="bank%d" % (PACK + i)) for i in range(PACK)]
+        for i in range(PACK):
+            nc.tensor.matmul_mx(
+                out=y_banks[i][:],
+                lhsT=wd_codes[:, i * P : (i + 1) * P].bitcast(E4M3),
+                lhsT_scale=wd_scale[:, i * P : (i + 1) * P],
+                rhs=g_codes[:].bitcast(E5M2),
+                rhs_scale=g_scale[:],
+                start=True,
                 stop=True,
             )
 
@@ -198,22 +214,21 @@ def tile_mix_gradient_clipped_between_pl_kernel(
         scale_on_scalar(1, 0)
         scale_on_scalar(0, 2)
         clip(0, 0)
-        clip(0, 1)
         scale_on_vector(0, 3)
         scale_on_scalar(1, 1)
         scale_on_scalar(1, 2)
         scale_on_scalar(1, 3)
+        clip(0, 1)
         clip(0, 2)
         clip(0, 3)
         clip(1, 0)
         interleave(nc.vector.tensor_copy, dc_bf[0], dc_rows[0], 0, HALF)
         clip(1, 1)
-        quantize_dc(0)
         clip(1, 2)
         clip(1, 3)
+        quantize_dc(0)
 
-        def last_product(h):
-            banks = [ps.tile([P, T], F32, name="y%d%d" % (h, i), tag="bank%d" % (PACK * (1 - h) + i)) for i in range(PACK)]
+        def last_product(h, banks):
             cols = slice(h * HALF, h * HALF + T)
             for i in range(PACK):
                 nc.tensor.matmul_mx(
@@ -241,17 +256,18 @@ def tile_mix_gradient_clipped_between_pl_kernel(
 
         def hand_on(h):
             cols = slice(h * HALF, (h + 1) * HALF)
-            interleave(nc.vector.tensor_copy, y_bf[h], y_rows[h], 0, HALF)
             nc.vector.quantize_mx(out=y_codes[h][:].bitcast(E4M3), scales=y_scale[:, cols], in_=y_bf[h][:])
             nc.sync.dma_start(out=out_words[:, cols], in_=y_codes[h][:])
 
-        first = last_product(0)
-        interleave(nc.vector.tensor_copy, dc_bf[1], dc_rows[1], 0, HALF)
+        first = last_product(0, y_banks)
+        interleave_shared(dc_bf[1], dc_rows[1])
         quantize_dc(1)
-        second = last_product(1)
+        second = last_product(1, [ps.tile([P, T], F32, name="y1%d" % i, tag="bank%d" % i) for i in range(PACK)])
         empty_banks(0, first)
+        interleave(nc.vector.tensor_copy, y_bf[0], y_rows[0], 0, HALF)
         hand_on(0)
         empty_banks(1, second)
+        interleave_shared(y_bf[1], y_rows[1])
         hand_on(1)
         for q in range(4):
             engine = nc.scalar if q % 2 else nc.sync

@@ -165,7 +165,7 @@ def tile_mix_gradient_clipped_between_pl_kernel(
         nc.scalar.activation(out=lower[:], in_=upper[:], func=ACT.Copy, scale=-1.0)
 
         y_banks = [ps.tile([P, T], F32, name="y0%d" % i, tag="bank%d" % (PACK + i)) for i in range(PACK)]
-        for i in range(PACK):
+        for i in (0, 1, 2, 3, 0, 1):
             nc.tensor.matmul_mx(
                 out=y_banks[i][:],
                 lhsT=wd_codes[:, i * P : (i + 1) * P].bitcast(E4M3),
@@ -249,10 +249,12 @@ def tile_mix_gradient_clipped_between_pl_kernel(
         out_rows = out_0.rearrange("(p i) t -> p i t", i=PACK)
         out_words = out_1[0].rearrange("p c j -> p (c j)").bitcast(I32)
 
-        def empty_banks(h, banks):
+        def empty_banks(h, banks, rows_per_store):
             for i in range(PACK):
                 nc.scalar.copy(out=y_rows[h][:, i, :], in_=banks[i][:, HALF:])
-            nc.sync.dma_start(out=out_rows[:, :, h * HALF : (h + 1) * HALF], in_=y_rows[h][:])
+                if (i + 1) % rows_per_store == 0:
+                    rows = slice(i + 1 - rows_per_store, i + 1)
+                    nc.sync.dma_start(out=out_rows[:, rows, h * HALF : (h + 1) * HALF], in_=y_rows[h][:, rows, :])
 
         def hand_on(h):
             cols = slice(h * HALF, (h + 1) * HALF)
@@ -263,14 +265,28 @@ def tile_mix_gradient_clipped_between_pl_kernel(
         interleave_shared(dc_bf[1], dc_rows[1])
         quantize_dc(1)
         second = last_product(1, [ps.tile([P, T], F32, name="y1%d" % i, tag="bank%d" % i) for i in range(PACK)])
-        empty_banks(0, first)
+        empty_banks(0, first, 1)
+        quarter = HALF // 2
+        for i in range(PACK - 1):
+            nc.scalar.copy(out=y_rows[1][:, i, :], in_=second[i][:, HALF:])
+            if i == 1:
+                nc.sync.dma_start(out=out_rows[:, :2, HALF:], in_=y_rows[1][:, :2, :])
+        nc.scalar.copy(out=y_rows[1][:, PACK - 1, :quarter], in_=second[PACK - 1][:, HALF : HALF + quarter])
+        nc.scalar.copy(out=y_rows[1][:, PACK - 1, quarter:], in_=second[PACK - 1][:, HALF + quarter :])
+        nc.sync.dma_start(out=out_rows[:, 2:, HALF:], in_=y_rows[1][:, 2:, :])
         interleave(nc.vector.tensor_copy, y_bf[0], y_rows[0], 0, HALF)
         hand_on(0)
-        empty_banks(1, second)
-        interleave_shared(y_bf[1], y_rows[1])
-        hand_on(1)
+        interleave(nc.vector.tensor_copy, y_bf[1], y_rows[1], 0, quarter)
+        interleave(nc.scalar.copy, y_bf[1], y_rows[1], quarter, HALF)
+        for c0 in (0, quarter):
+            nc.vector.quantize_mx(
+                out=y_codes[1][:, c0 : c0 + quarter].bitcast(E4M3),
+                scales=y_scale[:, HALF + c0 : HALF + c0 + quarter],
+                in_=y_bf[1][:, PACK * c0 : PACK * (c0 + quarter)],
+            )
+        nc.sync.dma_start(out=out_words[:, HALF:], in_=y_codes[1][:])
         for q in range(4):
-            engine = nc.scalar if q % 2 else nc.sync
+            engine = nc.sync if q == 3 else nc.scalar
             engine.dma_start(
                 out=out_2[0, 4 * q : 4 * q + 4, :].bitcast(I32),
                 in_=y_scale[32 * q : 32 * q + 4, :].bitcast(I32),

@@ -49,10 +49,10 @@ def tile_mix_gradient_clipped_between_pl_kernel(
                 in_=src[:, :, c0:c1].rearrange("p j (c i) -> p c j i", i=RUN),
             )
 
-        def deal_words(dst, src):
+        def deal_words(dst, src, tiles=slice(0, PACK)):
             nc.vector.tensor_copy(
-                out=dst.rearrange("p (j c i) -> p c j i", j=PACK, i=RUN),
-                in_=src.rearrange("p (c i j) -> p c j i", j=PACK, i=RUN),
+                out=dst.rearrange("p (j c i) -> p c j i", j=PACK, i=RUN)[:, :, tiles, :],
+                in_=src.rearrange("p (c i j) -> p c j i", j=PACK, i=RUN)[:, :, tiles, :],
             )
 
         def deal_scales(dst, src):
@@ -99,8 +99,8 @@ def tile_mix_gradient_clipped_between_pl_kernel(
             load_scale_rows(nc.sync, wd_scale_raw, wd_scales, q)
         nc.sync.dma_start(out=g_raw[1][:], in_=g_rows[:, :, HALF:])
         nc.sync.dma_start(out=wd_raw[:], in_=wd_words[0].rearrange("p c j -> p (c j)").bitcast(I32))
-        nc.sync.dma_start(out=us_cols[:], in_=us.rearrange("(p j) o -> p (j o)", j=PACK))
         nc.sync.dma_start(out=wu_raw[:].bitcast(I32), in_=wu_words[0].bitcast(I32))
+        nc.sync.dma_start(out=us_cols[:], in_=us.rearrange("(p j) o -> p (j o)", j=PACK))
         for q in range(4):
             load_scale_rows(nc.sync, wu_scale_raw, wu_scales, q)
 
@@ -145,8 +145,9 @@ def tile_mix_gradient_clipped_between_pl_kernel(
         deal_scales(wd_scale[:], wd_scale_raw[:])
         quantize_g(0)
         interleave_shared(g_bf[1], g_raw[1])
-        deal_words(wd_codes[:], wd_raw[:])
+        deal_words(wd_codes[:], wd_raw[:], slice(0, 2))
         quantize_g(1)
+        deal_words(wd_codes[:], wd_raw[:], slice(2, PACK))
 
         for j in range(PACK):
             nc.tensor.matmul_mx(
@@ -165,16 +166,6 @@ def tile_mix_gradient_clipped_between_pl_kernel(
         nc.scalar.activation(out=lower[:], in_=upper[:], func=ACT.Copy, scale=-1.0)
 
         y_banks = [ps.tile([P, T], F32, name="y0%d" % i, tag="bank%d" % (PACK + i)) for i in range(PACK)]
-        for i in (0, 1, 2, 3, 0, 1):
-            nc.tensor.matmul_mx(
-                out=y_banks[i][:],
-                lhsT=wd_codes[:, i * P : (i + 1) * P].bitcast(E4M3),
-                lhsT_scale=wd_scale[:, i * P : (i + 1) * P],
-                rhs=g_codes[:].bitcast(E5M2),
-                rhs_scale=g_scale[:],
-                start=True,
-                stop=True,
-            )
 
         wu_scale = tile("wu_scale", [P, K], U8)
         wu_codes = tile("wu_codes", [P, 2 * K], U8)

@@ -166,6 +166,16 @@ def tile_mix_gradient_clipped_between_pl_kernel(
         nc.scalar.activation(out=lower[:], in_=upper[:], func=ACT.Copy, scale=-1.0)
 
         y_banks = [ps.tile([P, T], F32, name="y0%d" % i, tag="bank%d" % (PACK + i)) for i in range(PACK)]
+        for i in (0, 1, 2, 3, 0, 1):
+            nc.tensor.matmul_mx(
+                out=y_banks[i][:],
+                lhsT=wd_codes[:, i * P : (i + 1) * P].bitcast(E4M3),
+                lhsT_scale=wd_scale[:, i * P : (i + 1) * P],
+                rhs=g_codes[:].bitcast(E5M2),
+                rhs_scale=g_scale[:],
+                start=True,
+                stop=True,
+            )
 
         wu_scale = tile("wu_scale", [P, K], U8)
         wu_codes = tile("wu_codes", [P, 2 * K], U8)

from contextlib import ExitStack

import concourse.mybir as mybir

N, L, R, K, T = 512, 1024, 512, 512, 512
FLOPS = 2 * T * (N * R + L * R + R * K)

F32 = mybir.dt.float32
BF16 = mybir.dt.bfloat16
I32 = mybir.dt.int32
U8 = mybir.dt.uint8
E4M3 = mybir.dt.float8_e4m3fn_x4
E5M2 = mybir.dt.float8_e5m2_x4
E2M1 = mybir.dt.float4_e2m1fn_x4
ALU = mybir.AluOpType
ACT = mybir.ActivationFunctionType

P = 128
PACK = 4
HALF = T // 2
RUN = 4
G_VECTOR_COLS = 176


def tile_mix_gradient_clipped_between_pl_kernel(
    tc, g, wd_words, wd_scales, xq_words, xq_scales, ws_words, ws_scales, us, wu_words, wu_scales,
    out_0, out_1, out_2,
):
    nc = tc.nc

    with ExitStack() as ctx:
        sb = ctx.enter_context(tc.tile_pool(name="sb", bufs=1))
        ps = ctx.enter_context(tc.psum_pool(name="ps", bufs=1))
        ctx.enter_context(tc.manual_schedule())

        def tile(name, shape, dtype):
            return sb.tile(shape, dtype, name=name, align_bytes=64)

        def load_scale_rows(engine, plane, scales, q):
            passes = scales.shape[0]
            engine.dma_start(
                out=plane[32 * q : 32 * q + 4, :].bitcast(I32).rearrange("r (z c) -> r z c", z=passes),
                in_=scales[:, 4 * q : 4 * q + 4, :].bitcast(I32).rearrange("z r c -> r z c"),
            )

        def interleave(copy, dst, src, c0, c1):
            copy(
                out=dst[:, PACK * c0 : PACK * c1].rearrange("p (c i j) -> p c j i", i=RUN, j=PACK),
                in_=src[:, :, c0:c1].rearrange("p j (c i) -> p c j i", i=RUN),
            )

        def deal_words(dst, src, tiles=slice(0, PACK)):
            nc.vector.tensor_copy(
                out=dst.rearrange("p (j c i) -> p c j i", j=PACK, i=RUN)[:, :, tiles, :],
                in_=src.rearrange("p (c i j) -> p c j i", j=PACK, i=RUN)[:, :, tiles, :],
            )

        def deal_scales(dst, src):
            nc.vector.tensor_copy(
                out=dst.rearrange("p (z j m) -> p z j m", j=PACK, m=P),
                in_=src.rearrange("p (z m j) -> p z j m", j=PACK, m=P),
            )

        ws_scale_raw = tile("ws_scale_raw", [P, 2 * R], U8)
        xq_scale = tile("xq_scale", [P, 2 * T], U8)
        wd_scale_raw = tile("wd_scale_raw", [P, R], U8)
        wu_scale_raw = tile("wu_scale_raw", [P, K], U8)
        dc_codes = tile("dc_codes", [P, HALF + T], I32)
        dc_scale = tile("dc_scale", [P, HALF + T], U8)
        us_cols = tile("us_cols", [P, PACK], F32)
        ws_raw = tile("ws_raw", [P, 2 * R], I32)
        xq_codes = tile("xq_codes", [P, 4 * T], U8)
        wd_raw = tile("wd_raw", [P, R], I32)
        wu_raw = tile("wu_raw", [P, 2 * K], U8)
        g_raw = [tile("g_raw%d" % h, [P, PACK, HALF], F32) for h in range(2)]

        for plane in (ws_scale_raw, xq_scale, wd_scale_raw, wu_scale_raw):
            nc.vector.memset(plane[:].bitcast(I32), 0)
        nc.vector.memset(dc_codes[:, :HALF], 0)
        nc.vector.memset(dc_scale[:, :HALF].bitcast(I32), 0)

        nc.sync.dma_start(
            out=xq_codes[:].bitcast(I32).rearrange("p (z c) -> p z c", z=2),
            in_=xq_words.rearrange("z p b -> p z b").bitcast(I32),
        )
        for q in range(4):
            load_scale_rows(nc.scalar if q % 2 else nc.sync, ws_scale_raw, ws_scales, q)
        for q in range(2):
            load_scale_rows(nc.scalar if q % 2 else nc.sync, xq_scale, xq_scales, q)
        nc.sync.dma_start(
            out=ws_raw[:].rearrange("p (z c) -> p z c", z=2),
            in_=ws_words.rearrange("z p c j -> p z (c j)").bitcast(I32),
        )
        for q in range(2, 4):
            load_scale_rows(nc.sync, xq_scale, xq_scales, q)
        g_rows = g.rearrange("(p j) t -> p j t", j=PACK)
        nc.sync.dma_start(out=g_raw[0][:], in_=g_rows[:, :, :HALF])
        for q in range(4):
            load_scale_rows(nc.sync, wd_scale_raw, wd_scales, q)
        nc.sync.dma_start(out=g_raw[1][:], in_=g_rows[:, :, HALF:])
        nc.sync.dma_start(out=wd_raw[:], in_=wd_words[0].rearrange("p c j -> p (c j)").bitcast(I32))
        nc.sync.dma_start(out=wu_raw[:].bitcast(I32), in_=wu_words[0].bitcast(I32))
        nc.sync.dma_start(out=us_cols[:], in_=us.rearrange("(p j) o -> p (j o)", j=PACK))
        for q in range(4):
            load_scale_rows(nc.sync, wu_scale_raw, wu_scales, q)

        ws_scale = tile("ws_scale", [P, 2 * R], U8)
        deal_scales(ws_scale[:], ws_scale_raw[:])
        ws_codes = [tile("ws_codes%d" % z, [P, R], I32) for z in range(2)]
        for z in range(2):
            deal_words(ws_codes[z][:], ws_raw[:, z * R : (z + 1) * R])

        d = [ps.tile([P, T], F32, name="d%d" % j, tag="bank%d" % j) for j in range(PACK)]
        for z in range(2):
            for j in range(PACK):
                nc.tensor.matmul_mx(
                    out=d[j][:],
                    lhsT=ws_codes[z][:, j * P : (j + 1) * P].bitcast(E4M3),
                    lhsT_scale=ws_scale[:, z * R + j * P : z * R + (j + 1) * P],
                    rhs=xq_codes[:, 2 * z * T : 2 * (z + 1) * T].bitcast(E2M1),
                    rhs_scale=xq_scale[:, z * T : (z + 1) * T],
                    start=(z == 0),
                    stop=False,
                )

        g_bf = [tile("g_bf%d" % h, [P, PACK * HALF], BF16) for h in range(2)]
        g_codes = tile("g_codes", [P, T], I32)
        g_scale = tile("g_scale", [P, T], U8)
        wd_scale = tile("wd_scale", [P, R], U8)
        wd_codes = tile("wd_codes", [P, R], I32)

        def cast_on_scalar(out, in_):
            nc.scalar.activation(out=out, in_=in_, func=ACT.Copy)

        def interleave_shared(dst, src):
            interleave(nc.vector.tensor_copy, dst, src, 0, G_VECTOR_COLS)
            interleave(nc.scalar.copy, dst, src, G_VECTOR_COLS, HALF)

        def quantize_g(h):
            cols = slice(h * HALF, (h + 1) * HALF)
            nc.vector.quantize_mx(out=g_codes[:, cols].bitcast(E5M2), scales=g_scale[:, cols], in_=g_bf[h][:])

        interleave(nc.vector.tensor_copy, g_bf[0], g_raw[0], 0, G_VECTOR_COLS)
        interleave(cast_on_scalar, g_bf[0], g_raw[0], G_VECTOR_COLS, HALF)
        deal_scales(wd_scale[:], wd_scale_raw[:])
        quantize_g(0)
        interleave_shared(g_bf[1], g_raw[1])
        deal_words(wd_codes[:], wd_raw[:], slice(0, 2))
        quantize_g(1)
        deal_words(wd_codes[:], wd_raw[:], slice(2, PACK))

        for j in range(PACK):
            nc.tensor.matmul_mx(
                out=d[j][:],
                lhsT=wd_codes[:, j * P : (j + 1) * P].bitcast(E4M3),
                lhsT_scale=wd_scale[:, j * P : (j + 1) * P],
                rhs=g_codes[:].bitcast(E5M2),
                rhs_scale=g_scale[:],
                start=False,
                stop=True,
            )

        upper = tile("upper", [P, PACK], F32)
        lower = tile("lower", [P, PACK], F32)
        nc.scalar.activation(out=upper[:], in_=us_cols[:], func=ACT.Abs)
        nc.scalar.activation(out=lower[:], in_=upper[:], func=ACT.Copy, scale=-1.0)

        y_banks = [ps.tile([P, T], F32, name="y0%d" % i, tag="bank%d" % (PACK + i)) for i in range(PACK)]
        for i in (0, 1, 2, 3, 0, 1):
            nc.tensor.matmul_mx(
                out=y_banks[i][:],
                lhsT=wd_codes[:, i * P : (i + 1) * P].bitcast(E4M3),
                lhsT_scale=wd_scale[:, i * P : (i + 1) * P],
                rhs=g_codes[:].bitcast(E5M2),
                rhs_scale=g_scale[:],
                start=True,
                stop=True,
            )

        wu_scale = tile("wu_scale", [P, K], U8)
        wu_codes = tile("wu_codes", [P, 2 * K], U8)
        nc.vector.tensor_copy(
            out=wu_codes[:].rearrange("p (j m b) -> p j m b", j=PACK, b=2),
            in_=wu_raw[:].rearrange("p (m j b) -> p j m b", j=PACK, b=2),
        )
        deal_scales(wu_scale[:], wu_scale_raw[:])

        product = [[tile("product%d%d" % (h, j), [P, HALF], BF16) for j in range(PACK)] for h in range(2)]
        dc_rows = [tile("dc_rows%d" % h, [P, PACK, HALF], BF16) for h in range(2)]
        dc_bf = [tile("dc_bf%d" % h, [P, PACK * HALF], BF16) for h in range(2)]

        def scale_on_scalar(h, j):
            nc.scalar.activation(
                out=product[h][j][:], in_=d[j][:, h * HALF : (h + 1) * HALF], func=ACT.Copy, scale=us_cols[:, j : j + 1]
            )

        def scale_on_vector(h, j):
            nc.vector.tensor_scalar(
                out=product[h][j][:], in0=d[j][:, h * HALF : (h + 1) * HALF],
                scalar1=us_cols[:, j : j + 1], scalar2=None, op0=ALU.mult,
            )

        def clip(h, j):
            nc.vector.tensor_scalar(
                out=dc_rows[h][:, j, :], in0=product[h][j][:],
                scalar1=upper[:, j : j + 1], scalar2=lower[:, j : j + 1], op0=ALU.min, op1=ALU.max,
            )

        def quantize_dc(h):
            cols = slice((h + 1) * HALF, (h + 2) * HALF)
            nc.vector.quantize_mx(out=dc_codes[:, cols].bitcast(E5M2), scales=dc_scale[:, cols], in_=dc_bf[h][:])

        scale_on_scalar(0, 0)
        scale_on_vector(0, 1)
        scale_on_scalar(1, 0)
        scale_on_scalar(0, 2)
        clip(0, 0)
        scale_on_vector(0, 3)
        scale_on_scalar(1, 1)
        scale_on_scalar(1, 2)
        scale_on_scalar(1, 3)
        clip(0, 1)
        clip(0, 2)
        clip(0, 3)
        clip(1, 0)
        interleave(nc.vector.tensor_copy, dc_bf[0], dc_rows[0], 0, HALF)
        clip(1, 1)
        clip(1, 2)
        clip(1, 3)
        quantize_dc(0)

        def last_product(h, banks):
            cols = slice(h * HALF, h * HALF + T)
            for i in range(PACK):
                nc.tensor.matmul_mx(
                    out=banks[i][:],
                    lhsT=wu_codes[:, 2 * i * P : 2 * (i + 1) * P].bitcast(E2M1),
                    lhsT_scale=wu_scale[:, i * P : (i + 1) * P],
                    rhs=dc_codes[:, cols].bitcast(E5M2),
                    rhs_scale=dc_scale[:, cols],
                    start=True,
                    stop=True,
                )
            return banks

        y_rows = [tile("y_rows%d" % h, [P, PACK, HALF], F32) for h in range(2)]
        y_bf = [tile("y_bf%d" % h, [P, PACK * HALF], BF16) for h in range(2)]
        y_codes = [tile("y_codes%d" % h, [P, HALF], I32) for h in range(2)]
        y_scale = tile("y_scale", [P, T], U8)
        out_rows = out_0.rearrange("(p i) t -> p i t", i=PACK)
        out_words = out_1[0].rearrange("p c j -> p (c j)").bitcast(I32)

        def empty_banks(h, banks, rows_per_store):
            for i in range(PACK):
                nc.scalar.copy(out=y_rows[h][:, i, :], in_=banks[i][:, HALF:])
                if (i + 1) % rows_per_store == 0:
                    rows = slice(i + 1 - rows_per_store, i + 1)
                    nc.sync.dma_start(out=out_rows[:, rows, h * HALF : (h + 1) * HALF], in_=y_rows[h][:, rows, :])

        def hand_on(h):
            cols = slice(h * HALF, (h + 1) * HALF)
            nc.vector.quantize_mx(out=y_codes[h][:].bitcast(E4M3), scales=y_scale[:, cols], in_=y_bf[h][:])
            nc.sync.dma_start(out=out_words[:, cols], in_=y_codes[h][:])

        first = last_product(0, y_banks)
        interleave_shared(dc_bf[1], dc_rows[1])
        quantize_dc(1)
        second = last_product(1, [ps.tile([P, T], F32, name="y1%d" % i, tag="bank%d" % i) for i in range(PACK)])
        empty_banks(0, first, 1)
        quarter = HALF // 2
        for i in range(PACK - 1):
            nc.scalar.copy(out=y_rows[1][:, i, :], in_=second[i][:, HALF:])
            if i == 1:
                nc.sync.dma_start(out=out_rows[:, :2, HALF:], in_=y_rows[1][:, :2, :])
        nc.scalar.copy(out=y_rows[1][:, PACK - 1, :quarter], in_=second[PACK - 1][:, HALF : HALF + quarter])
        nc.scalar.copy(out=y_rows[1][:, PACK - 1, quarter:], in_=second[PACK - 1][:, HALF + quarter :])
        nc.sync.dma_start(out=out_rows[:, 2:, HALF:], in_=y_rows[1][:, 2:, :])
        interleave(nc.vector.tensor_copy, y_bf[0], y_rows[0], 0, HALF)
        hand_on(0)
        interleave(nc.vector.tensor_copy, y_bf[1], y_rows[1], 0, quarter)
        interleave(nc.scalar.copy, y_bf[1], y_rows[1], quarter, HALF)
        for c0 in (0, quarter):
            nc.vector.quantize_mx(
                out=y_codes[1][:, c0 : c0 + quarter].bitcast(E4M3),
                scales=y_scale[:, HALF + c0 : HALF + c0 + quarter],
                in_=y_bf[1][:, PACK * c0 : PACK * (c0 + quarter)],
            )
        nc.sync.dma_start(out=out_words[:, HALF:], in_=y_codes[1][:])
        for q in range(4):
            engine = nc.sync if q == 3 else nc.scalar
            engine.dma_start(
                out=out_2[0, 4 * q : 4 * q + 4, :].bitcast(I32),
                in_=y_scale[32 * q : 32 * q + 4, :].bitcast(I32),
            )
